import numpy as np
import ml_dtypes


def mxq(x, axis, fmt="e4m3"):
    dtype, down = {"e4m3": (ml_dtypes.float8_e4m3fn, 7), "e5m2": (ml_dtypes.float8_e5m2, 14)}[fmt]
    v = np.moveaxis(np.asarray(x, np.float32).astype(ml_dtypes.bfloat16).astype(np.float64), axis, -1)
    blocks = v.reshape(v.shape[:-1] + (-1, 32))
    amax = np.abs(blocks).max(-1, keepdims=True)
    byte = np.maximum(np.where(amax > 0, np.frexp(amax)[1] - 1 + 127, 0) - down, 1)
    scale = np.exp2(byte - 127.0)
    codes = (blocks / scale).astype(np.float32).astype(dtype).astype(np.float64)
    return np.moveaxis((codes * scale).reshape(v.shape), -1, axis)


WIDE = False


def mx_kscale(k):
    if not WIDE:
        return np.ones(k)
    levels = np.array([10, -10, 5, -5, 0])
    if k % 512:
        return np.exp2(np.random.permutation(np.resize(levels, k // 32))).repeat(32)
    a = np.empty((k // 512, 16))
    for p in range(k // 512):
        a[p, :8] = np.random.permutation(np.resize(levels, 8))
        for g in range(8):
            far = levels[np.abs(levels - a[p, g]) >= 10]
            a[p, g + 8] = far[np.random.randint(len(far))]
    return np.exp2(a.ravel()).repeat(32)


def f64(x):
    return np.asarray(x).astype(np.float64)


def striped(idx):
    return np.tile(idx.reshape(-1, 16).T, (8, 1)).astype(np.uint16)


def unstriped(offs):
    return offs[:16].T.reshape(-1).astype(np.int64)


def pack_weight(w):
    k, n = w.shape
    w = f64(np.asarray(w, np.float32).astype(ml_dtypes.bfloat16)).reshape(k // 32, 32, n)
    amax = np.abs(w).max(1)
    byte = np.clip(np.where(amax > 0, np.frexp(amax)[1] - 1 + 127 - 7, 1), 1, 254)
    scaled = (w * np.exp2(127.0 - byte)[:, None, :]).reshape(k, n).astype(np.float32)
    words = np.ascontiguousarray(scaled.reshape(k // 512, 128, 4, n).transpose(0, 1, 3, 2)).astype(ml_dtypes.float8_e4m3fn).view(np.uint8)
    return words, np.ascontiguousarray(byte.astype(np.uint8).reshape(k // 512, 16, n))


def unpack_weight(words, scales):
    g, p, n, _ = words.shape
    vals = np.ascontiguousarray(words).view(ml_dtypes.float8_e4m3fn).astype(np.float64) * np.repeat(np.exp2(scales.astype(np.float64) - 127.0), 8, axis=1)[..., None]
    return vals.transpose(0, 1, 3, 2).reshape(g * 512, n)


def sigmoid(v):
    return 1.0 / (1.0 + np.exp(-np.maximum(v, -700.0)))


def gelu(v):
    return 0.5 * v * (1.0 + np.tanh(np.sqrt(2.0 / np.pi) * (v + 0.044715 * v**3)))


K, T, S, N, H, W, U = 512, 1024, 512, 128, 512, 2048, 1024


def setup_inputs():
    n = np.random.standard_normal
    s = mx_kscale(K)[:, None]
    u = mx_kscale(H)
    packed_xT = pack_weight(n((K, T)) * s)
    packed_eT = pack_weight(n((K, W)) * s)
    return {
        "x_words": packed_xT[0],
        "x_scales": packed_xT[1],
        "w1": (n((K, H)) / np.sqrt(K) / s).astype(np.float32),
        "e_words": packed_eT[0],
        "e_scales": packed_eT[1],
        "w2": (n((K, H)) / np.sqrt(K) / s).astype(np.float32),
        "mod": (np.random.uniform(0.4, 1.6, (H, U))).astype(np.float32),
        "unit": (np.random.uniform(0.6, 1.4, (H, 1)) * u[:, None]).astype(np.float32),
        "w3": (n((H, N)) / np.sqrt(H) / u[:, None]).astype(np.float32),
        "res": (n((N, U))).astype(np.float32),
        "offs": striped(np.random.permutation(T)[:S]),
        "nxt": striped(np.random.permutation(W)[:S]),
        "par": striped(np.random.permutation(np.concatenate([np.arange(S), np.random.randint(0, S, U - S)]))),
    }


def reference(x_words, x_scales, w1, e_words, e_scales, w2, mod, unit, w3, res, offs, nxt, par):
    xq = unpack_weight(x_words, x_scales)[:, unstriped(offs)]
    y = mxq(f64(w1), 0, "e4m3").T @ xq
    e_nxt = unpack_weight(e_words, e_scales)[:, unstriped(nxt)]
    ye = mxq(f64(w2), 0, "e4m3").T @ e_nxt
    jn = gelu(y + ye)
    mu = jn.mean(axis=1, keepdims=True)
    cn = jn - mu
    c2 = (cn) ** 2
    va = c2.mean(axis=1, keepdims=True)
    nr = cn / np.sqrt(va + 0.1)
    vp = nr[:, unstriped(par)]
    hid = f64(unit) * (vp * f64(mod))
    rr = mxq(f64(w3), 0, "e4m3").T @ mxq(hid, 0, "e4m3")
    return f64(res) + rr * (sigmoid(2.0 * f64(res)))

@@ -1,0 +1,216 @@
+from contextlib import ExitStack
+
+import concourse.mybir as mybir
+
+K, T, S, N, H, W, U = 512, 1024, 512, 128, 512, 2048, 1024
+FLOPS = 2 * K * H * S * 2 + 2 * H * N * U
+
+F32 = mybir.dt.float32
+BF16 = mybir.dt.bfloat16
+I32 = mybir.dt.int32
+U32 = mybir.dt.uint32
+U16 = mybir.dt.uint16
+U8 = mybir.dt.uint8
+FP8X4 = mybir.dt.float8_e4m3fn_x4
+ALU = mybir.AluOpType
+ACT = mybir.ActivationFunctionType
+
+P = 128
+PACK = 4
+EPS = 0.1
+CHUNKS = (256, 256, 256, 128, 128)
+VECTOR_SHARE = 40
+
+
+def tile_picked_ymtph_gate_p_kernel(tc, x_words, x_scales, w1, e_words, e_scales, w2, mod, unit, w3, res, offs, nxt, par, out):
+    nc = tc.nc
+    with ExitStack() as ctx:
+        keep = ctx.enter_context(tc.tile_pool(name="keep", bufs=1))
+        psum = ctx.enter_context(tc.psum_pool(name="psum", bufs=1))
+        psum_out = ctx.enter_context(tc.psum_pool(name="psum_out", bufs=4))
+
+        offs_sb = keep.tile([P, S // 16], U16, name="offs_sb")
+        nxt_sb = keep.tile([P, S // 16], U16, name="nxt_sb")
+        par_sb = keep.tile([P, U // 16], U16, name="par_sb")
+        xs_tab = keep.tile([P, T], U8, name="xs_tab", align_bytes=64)
+        es_tab = keep.tile([P, W], U8, name="es_tab", align_bytes=64)
+        xw_tab = keep.tile([P, T], U32, name="xw_tab", align_bytes=64)
+        ew_tab = keep.tile([P, W], U32, name="ew_tab", align_bytes=64)
+        w1_raw = [keep.tile([P, PACK, H // 2], F32, name=f"w1_raw{h}") for h in range(2)]
+        w2_raw = [keep.tile([P, PACK, H // 2], F32, name=f"w2_raw{h}") for h in range(2)]
+        w3_raw = keep.tile([P, PACK, N], F32, name="w3_raw")
+        unit_sb = keep.tile([P, PACK], F32, name="unit_sb")
+        mod_sb = [keep.tile([P, U], F32, name=f"mod_sb{t}") for t in range(PACK)]
+        res_sb = keep.tile([P, U], F32, name="res_sb")
+        minus_half = keep.tile([P, 2], F32, name="minus_half")
+
+        nc.gpsimd.memset(xs_tab[:].bitcast(I32), 0)
+        nc.vector.memset(es_tab[:].bitcast(I32), 0)
+        nc.gpsimd.memset(minus_half[:], -0.5)
+
+        def load_scales(tab, scales):
+            for q in range(4):
+                nc.sync.dma_start(out=tab[32 * q : 32 * q + 4, :].bitcast(I32), in_=scales[0, 4 * q : 4 * q + 4, :].bitcast(I32))
+
+        def load_words(tab, words):
+            nc.sync.dma_start(out=tab[:].bitcast(I32), in_=words[0].rearrange("p n j -> p (n j)").bitcast(I32))
+
+        def load_weight(halves, w):
+            rows = w.rearrange("(p j) c -> p j c", j=PACK)
+            for h in range(2):
+                nc.sync.dma_start(out=halves[h][:], in_=rows[:, :, h * H // 2 : (h + 1) * H // 2])
+
+        nc.sync.dma_start(out=offs_sb[:], in_=offs)
+        nc.sync.dma_start(out=nxt_sb[:], in_=nxt)
+        load_words(xw_tab, x_words)
+        load_scales(xs_tab, x_scales)
+        load_words(ew_tab, e_words)
+        load_scales(es_tab, e_scales)
+        load_weight(w1_raw, w1)
+        load_weight(w2_raw, w2)
+        nc.sync.dma_start(out=par_sb[:], in_=par)
+        nc.sync.dma_start(out=unit_sb[:], in_=unit.rearrange("(p t) o -> p (t o)", t=PACK))
+        mod_rows = mod.rearrange("(p t) r -> p t r", t=PACK)
+        for t in range(PACK):
+            nc.sync.dma_start(out=mod_sb[t][:], in_=mod_rows[:, t, :])
+        nc.sync.dma_start(out=w3_raw[:], in_=w3.rearrange("(p j) c -> p j c", j=PACK))
+        nc.sync.dma_start(out=res_sb[:], in_=res)
+
+        def gather_scales(tab, lst, name):
+            picked = keep.tile([P, S], U8, name=name, align_bytes=64)
+            nc.vector.tensor_copy(out=picked[:], in_=tab[:].indirect(lst[:]))
+            return picked
+
+        def gather_words(tab, lst, name):
+            picked = keep.tile([P, S], U32, name=name, align_bytes=64)
+            nc.vector.tensor_copy(out=picked[:], in_=tab[:].indirect(lst[:]))
+            return picked
+
+        def deal(halves, name, vector_shares):
+            grouped = keep.tile([P, PACK * H], BF16, name=name, align_bytes=64)
+            dealt = grouped[:].rearrange("p (t m j) -> p m j t", t=PACK, j=PACK)
+            for h in range(2):
+                dst = dealt[:, h * P // 2 : (h + 1) * P // 2]
+                src = halves[h][:].rearrange("p j (m t) -> p m j t", t=PACK)
+                share = vector_shares[h]
+                if share:
+                    nc.vector.tensor_copy(out=dst[:, :share], in_=src[:, :share])
+                nc.scalar.copy(out=dst[:, share:], in_=src[:, share:])
+            return grouped
+
+        def quantize(grouped, width, name):
+            codes = keep.tile([P, width], U32, name=name + "_codes", align_bytes=64)
+            scales = keep.tile([P, width], U8, name=name + "_scales", align_bytes=64)
+            nc.vector.quantize_mx(out=codes[:].bitcast(FP8X4), scales=scales[:], in_=grouped[:])
+            return codes, scales
+
+        xw = gather_words(xw_tab, offs_sb, "xw")
+        xs = gather_scales(xs_tab, offs_sb, "xs")
+        ew = gather_words(ew_tab, nxt_sb, "ew")
+        es = gather_scales(es_tab, nxt_sb, "es")
+        w1_grouped = deal(w1_raw, "w1_grouped", (0, VECTOR_SHARE))
+        w1_codes, w1_scales = quantize(w1_grouped, H, "w1")
+        w2_grouped = deal(w2_raw, "w2_grouped", (VECTOR_SHARE, VECTOR_SHARE))
+        w2_codes = keep.tile([P, H], U32, name="w2_codes", align_bytes=64)
+        w2_scales = keep.tile([P, H], U8, name="w2_scales", align_bytes=64)
+        for t in range(PACK):
+            cols = slice(P * t, P * (t + 1))
+            nc.vector.quantize_mx(out=w2_codes[:, cols].bitcast(FP8X4), scales=w2_scales[:, cols], in_=w2_grouped[:, H * t : H * (t + 1)])
+
+        pre = [psum.tile([P, S], F32, name=f"pre{t}") for t in range(PACK)]
+        for t in range(PACK):
+            cols = slice(P * t, P * (t + 1))
+            for codes, scales, words, byts, first in ((w1_codes, w1_scales, xw, xs, True), (w2_codes, w2_scales, ew, es, False)):
+                nc.tensor.matmul_mx(out=pre[t][:], lhsT=codes[:, cols].bitcast(FP8X4), lhsT_scale=scales[:, cols],
+                                    rhs=words[:].bitcast(FP8X4), rhs_scale=byts[:], start=first, stop=not first)
+
+        jn = [keep.tile([P, S], F32, name=f"jn{t}") for t in range(PACK)]
+        window = [keep.tile([P, S], F32, name=f"window{t}") for t in range(PACK)]
+        row_sum = keep.tile([P, 2], F32, name="row_sum")
+        minus_mean = keep.tile([P, 2], F32, name="minus_mean")
+        square_sum = keep.tile([P, 2], F32, name="square_sum")
+        squares = keep.tile([P, S], F32, name="squares")
+
+        def activate(t):
+            if t < 2:
+                nc.scalar.activation(out=jn[t][:], in_=pre[t][:], func=ACT.Gelu_apprx_tanh)
+            else:
+                nc.scalar.activation(out=jn[t][:], in_=pre[t][:], func=ACT.Gelu_apprx_tanh, accum_out=row_sum[:, t - 2 : t - 1])
+
+        def normalise_on_vector(t):
+            stats = keep.tile([P, 6], F32, name=f"stats{t}")
+            mean_var = keep.tile([P, 2], F32, name=f"mean_var{t}")
+            var_eps = keep.tile([P, 1], F32, name=f"var_eps{t}")
+            rstd = keep.tile([P, 1], F32, name=f"rstd{t}")
+            factor = keep.tile([P, 1], F32, name=f"factor{t}")
+            nc.vector.bn_stats(out=stats[:], in_=jn[t][:])
+            nc.vector.bn_aggr(out=mean_var[:], in_=stats[:])
+            nc.vector.tensor_scalar(out=var_eps[:], in0=mean_var[:, 1:2], scalar1=EPS, scalar2=None, op0=ALU.add)
+            nc.gpsimd.tensor_tensor(out=rstd[:], in0=var_eps[:], in1=minus_half[:, 0:1], op=ALU.pow)
+            nc.vector.tensor_tensor(out=factor[:], in0=rstd[:], in1=unit_sb[:, t : t + 1], op=ALU.mult)
+            nc.vector.tensor_scalar(out=window[t][:], in0=jn[t][:], scalar1=mean_var[:, 0:1], scalar2=factor[:], op0=ALU.subtract, op1=ALU.mult)
+
+        def normalise_on_scalar():
+            var_eps = keep.tile([P, 2], F32, name="var_eps23")
+            rstd = keep.tile([P, 2], F32, name="rstd23")
+            nc.scalar.activation(out=minus_mean[:], in_=row_sum[:], func=ACT.Copy, scale=-1.0 / S)
+            for u in range(2):
+                nc.scalar.activation(out=squares[:], in_=jn[2 + u][:], func=ACT.Square, bias=minus_mean[:, u : u + 1], accum_out=square_sum[:, u : u + 1])
+            nc.scalar.activation(out=var_eps[:], in_=square_sum[:], func=ACT.Copy, scale=1.0 / S, bias=EPS)
+            nc.gpsimd.tensor_tensor(out=rstd[:], in0=var_eps[:], in1=minus_half[:], op=ALU.pow)
+            factor = keep.tile([P, 2], F32, name="factor23")
+            shift = keep.tile([P, 2], F32, name="shift23")
+            for u in range(2):
+                nc.scalar.activation(out=factor[:, u : u + 1], in_=unit_sb[:, 2 + u : 3 + u], func=ACT.Copy, scale=rstd[:, u : u + 1])
+            for u in range(2):
+                nc.scalar.activation(out=shift[:, u : u + 1], in_=minus_mean[:, u : u + 1], func=ACT.Copy, scale=factor[:, u : u + 1])
+            for u in range(2):
+                nc.scalar.activation(out=window[2 + u][:], in_=jn[2 + u][:], func=ACT.Identity, scale=factor[:, u : u + 1], bias=shift[:, u : u + 1])
+
+        for t in range(PACK):
+            activate(t)
+        normalise_on_vector(0)
+        normalise_on_vector(1)
+        normalise_on_scalar()
+
+        w3_grouped = keep.tile([P, N * PACK], BF16, name="w3_grouped", align_bytes=64)
+        nc.scalar.copy(out=w3_grouped[:].rearrange("p (c i j) -> p c j i", i=4, j=PACK), in_=w3_raw[:].rearrange("p j (c i) -> p c j i", i=4))
+        w3_codes, w3_scales = quantize(w3_grouped, N, "w3")
+        gate = keep.tile([P, U], F32, name="gate")
+
+        starts = [sum(CHUNKS[:c]) for c in range(len(CHUNKS))]
+        grouped = {}
+        product = {}
+
+        def fetch(c):
+            r0, n = starts[c], CHUNKS[c]
+            hid = keep.tile([P, PACK, n], F32, name=f"hid{c}")
+            for t in range(PACK):
+                nc.vector.tensor_tensor(out=hid[:, t, :], in0=window[t][:].indirect(par_sb[:, r0 // 16 : (r0 + n) // 16]),
+                                        in1=mod_sb[t][:, r0 : r0 + n], op=ALU.mult)
+            grouped[c] = keep.tile([P, n * PACK], BF16, name=f"hid_grouped{c}", align_bytes=64)
+            nc.scalar.copy(out=grouped[c][:].rearrange("p (c i t) -> p c t i", i=4, t=PACK), in_=hid[:].rearrange("p t (c i) -> p c t i", i=4))
+            nc.scalar.activation(out=gate[:, r0 : r0 + n], in_=res_sb[:, r0 : r0 + n], func=ACT.Tanh)
+
+        def project(c):
+            n = CHUNKS[c]
+            codes, scales = quantize(grouped[c], n, f"hid{c}")
+            product[c] = psum_out.tile([P, n], F32, name="rr")
+            nc.tensor.matmul_mx(out=product[c][:], lhsT=w3_codes[:].bitcast(FP8X4), lhsT_scale=w3_scales[:],
+                                rhs=codes[:].bitcast(FP8X4), rhs_scale=scales[:], start=True, stop=True)
+
+        def finish(c):
+            r0, n = starts[c], CHUNKS[c]
+            gated = keep.tile([P, n], F32, name=f"gated{c}")
+            result = keep.tile([P, n], F32, name=f"result{c}")
+            nc.vector.scalar_tensor_tensor(out=gated[:], in0=gate[:, r0 : r0 + n], scalar=1.0, in1=product[c][:], op0=ALU.add, op1=ALU.mult)
+            nc.vector.scalar_tensor_tensor(out=result[:], in0=gated[:], scalar=0.5, in1=res_sb[:, r0 : r0 + n], op0=ALU.mult, op1=ALU.add)
+            nc.sync.dma_start(out=out[:, r0 : r0 + n], in_=result[:])
+
+        for step in range(len(CHUNKS) + 2):
+            if step < len(CHUNKS):
+                fetch(step)
+            if 1 <= step <= len(CHUNKS):
+                project(step - 1)
+            if step >= 2:
+                finish(step - 2)

@@ -18,7 +18,8 @@ ACT = mybir.ActivationFunctionType
 P = 128
 PACK = 4
 EPS = 0.1
-CHUNKS = (256, 256, 256, 128, 128)
+CHUNKS = (512, 384, 128)
+SPARE = 32
 VECTOR_SHARE = 40
 
 
@@ -27,7 +28,7 @@ def tile_picked_ymtph_gate_p_kernel(tc, x_words, x_scales, w1, e_words, e_scales
     with ExitStack() as ctx:
         keep = ctx.enter_context(tc.tile_pool(name="keep", bufs=1))
         psum = ctx.enter_context(tc.psum_pool(name="psum", bufs=1))
-        psum_out = ctx.enter_context(tc.psum_pool(name="psum_out", bufs=4))
+        psum_out = ctx.enter_context(tc.psum_pool(name="psum_out", bufs=3))
 
         offs_sb = keep.tile([P, S // 16], U16, name="offs_sb")
         nxt_sb = keep.tile([P, S // 16], U16, name="nxt_sb")
@@ -64,16 +65,16 @@ def tile_picked_ymtph_gate_p_kernel(tc, x_words, x_scales, w1, e_words, e_scales
         nc.sync.dma_start(out=nxt_sb[:], in_=nxt)
         load_words(xw_tab, x_words)
         load_scales(xs_tab, x_scales)
-        load_words(ew_tab, e_words)
-        load_scales(es_tab, e_scales)
         load_weight(w1_raw, w1)
+        load_scales(es_tab, e_scales)
+        load_words(ew_tab, e_words)
         load_weight(w2_raw, w2)
-        nc.sync.dma_start(out=par_sb[:], in_=par)
         nc.sync.dma_start(out=unit_sb[:], in_=unit.rearrange("(p t) o -> p (t o)", t=PACK))
+        nc.sync.dma_start(out=w3_raw[:], in_=w3.rearrange("(p j) c -> p j c", j=PACK))
+        nc.sync.dma_start(out=par_sb[:], in_=par)
         mod_rows = mod.rearrange("(p t) r -> p t r", t=PACK)
         for t in range(PACK):
             nc.sync.dma_start(out=mod_sb[t][:], in_=mod_rows[:, t, :])
-        nc.sync.dma_start(out=w3_raw[:], in_=w3.rearrange("(p j) c -> p j c", j=PACK))
         nc.sync.dma_start(out=res_sb[:], in_=res)
 
         def gather_scales(tab, lst, name):
@@ -106,10 +107,10 @@ def tile_picked_ymtph_gate_p_kernel(tc, x_words, x_scales, w1, e_words, e_scales
 
         xw = gather_words(xw_tab, offs_sb, "xw")
         xs = gather_scales(xs_tab, offs_sb, "xs")
-        ew = gather_words(ew_tab, nxt_sb, "ew")
+        w1_grouped = deal(w1_raw, "w1_grouped", (0, 0))
         es = gather_scales(es_tab, nxt_sb, "es")
-        w1_grouped = deal(w1_raw, "w1_grouped", (0, VECTOR_SHARE))
         w1_codes, w1_scales = quantize(w1_grouped, H, "w1")
+        ew = gather_words(ew_tab, nxt_sb, "ew")
         w2_grouped = deal(w2_raw, "w2_grouped", (VECTOR_SHARE, VECTOR_SHARE))
         w2_codes = keep.tile([P, H], U32, name="w2_codes", align_bytes=64)
         w2_scales = keep.tile([P, H], U8, name="w2_scales", align_bytes=64)
@@ -124,59 +125,60 @@ def tile_picked_ymtph_gate_p_kernel(tc, x_words, x_scales, w1, e_words, e_scales
                 nc.tensor.matmul_mx(out=pre[t][:], lhsT=codes[:, cols].bitcast(FP8X4), lhsT_scale=scales[:, cols],
                                     rhs=words[:].bitcast(FP8X4), rhs_scale=byts[:], start=first, stop=not first)
 
-        jn = [keep.tile([P, S], F32, name=f"jn{t}") for t in range(PACK)]
-        window = [keep.tile([P, S], F32, name=f"window{t}") for t in range(PACK)]
-        row_sum = keep.tile([P, 2], F32, name="row_sum")
-        minus_mean = keep.tile([P, 2], F32, name="minus_mean")
-        square_sum = keep.tile([P, 2], F32, name="square_sum")
-        squares = keep.tile([P, S], F32, name="squares")
-
-        def activate(t):
-            if t < 2:
-                nc.scalar.activation(out=jn[t][:], in_=pre[t][:], func=ACT.Gelu_apprx_tanh)
-            else:
-                nc.scalar.activation(out=jn[t][:], in_=pre[t][:], func=ACT.Gelu_apprx_tanh, accum_out=row_sum[:, t - 2 : t - 1])
-
-        def normalise_on_vector(t):
-            stats = keep.tile([P, 6], F32, name=f"stats{t}")
-            mean_var = keep.tile([P, 2], F32, name=f"mean_var{t}")
-            var_eps = keep.tile([P, 1], F32, name=f"var_eps{t}")
-            rstd = keep.tile([P, 1], F32, name=f"rstd{t}")
-            factor = keep.tile([P, 1], F32, name=f"factor{t}")
-            nc.vector.bn_stats(out=stats[:], in_=jn[t][:])
-            nc.vector.bn_aggr(out=mean_var[:], in_=stats[:])
-            nc.vector.tensor_scalar(out=var_eps[:], in0=mean_var[:, 1:2], scalar1=EPS, scalar2=None, op0=ALU.add)
-            nc.gpsimd.tensor_tensor(out=rstd[:], in0=var_eps[:], in1=minus_half[:, 0:1], op=ALU.pow)
-            nc.vector.tensor_tensor(out=factor[:], in0=rstd[:], in1=unit_sb[:, t : t + 1], op=ALU.mult)
-            nc.vector.tensor_scalar(out=window[t][:], in0=jn[t][:], scalar1=mean_var[:, 0:1], scalar2=factor[:], op0=ALU.subtract, op1=ALU.mult)
-
-        def normalise_on_scalar():
-            var_eps = keep.tile([P, 2], F32, name="var_eps23")
-            rstd = keep.tile([P, 2], F32, name="rstd23")
-            nc.scalar.activation(out=minus_mean[:], in_=row_sum[:], func=ACT.Copy, scale=-1.0 / S)
-            for u in range(2):
-                nc.scalar.activation(out=squares[:], in_=jn[2 + u][:], func=ACT.Square, bias=minus_mean[:, u : u + 1], accum_out=square_sum[:, u : u + 1])
-            nc.scalar.activation(out=var_eps[:], in_=square_sum[:], func=ACT.Copy, scale=1.0 / S, bias=EPS)
-            nc.gpsimd.tensor_tensor(out=rstd[:], in0=var_eps[:], in1=minus_half[:], op=ALU.pow)
-            factor = keep.tile([P, 2], F32, name="factor23")
-            shift = keep.tile([P, 2], F32, name="shift23")
-            for u in range(2):
-                nc.scalar.activation(out=factor[:, u : u + 1], in_=unit_sb[:, 2 + u : 3 + u], func=ACT.Copy, scale=rstd[:, u : u + 1])
-            for u in range(2):
-                nc.scalar.activation(out=shift[:, u : u + 1], in_=minus_mean[:, u : u + 1], func=ACT.Copy, scale=factor[:, u : u + 1])
-            for u in range(2):
-                nc.scalar.activation(out=window[2 + u][:], in_=jn[2 + u][:], func=ACT.Identity, scale=factor[:, u : u + 1], bias=shift[:, u : u + 1])
-
-        for t in range(PACK):
-            activate(t)
-        normalise_on_vector(0)
-        normalise_on_vector(1)
-        normalise_on_scalar()
-
         w3_grouped = keep.tile([P, N * PACK], BF16, name="w3_grouped", align_bytes=64)
         nc.scalar.copy(out=w3_grouped[:].rearrange("p (c i j) -> p c j i", i=4, j=PACK), in_=w3_raw[:].rearrange("p j (c i) -> p c j i", i=4))
         w3_codes, w3_scales = quantize(w3_grouped, N, "w3")
+
+        jn = [keep.tile([P, S], F32, name=f"jn{t}") for t in range(PACK)]
+        window = [keep.tile([P, S + SPARE], F32, name=f"window{t}") for t in range(PACK)]
+        for t in range(PACK):
+            nc.gpsimd.memset(window[t][:, S:], 0.0)
+        hid = [keep.tile([P, PACK, n], F32, name=f"hid{c}") for c, n in enumerate(CHUNKS)]
+        last = PACK - 1
+        row_sum = keep.tile([P, 1], F32, name="row_sum")
+        minus_mean = keep.tile([P, 1], F32, name="minus_mean")
+        square_sum = keep.tile([P, 1], F32, name="square_sum")
+        minus_unit = keep.tile([P, PACK], F32, name="minus_unit")
+        pair = keep.tile([P, PACK, 2], F32, name="pair")
+        affine = keep.tile([P, PACK, 2], F32, name="affine")
+        nc.scalar.activation(out=minus_unit[:], in_=unit_sb[:], func=ACT.Copy, scale=-1.0)
+        nc.scalar.copy(out=pair[:, :, 0], in_=unit_sb[:])
+
+        for t in range(last):
+            nc.scalar.activation(out=jn[t][:], in_=pre[t][:], func=ACT.Gelu_apprx_tanh)
+        nc.scalar.activation(out=jn[last][:], in_=pre[last][:], func=ACT.Gelu_apprx_tanh, accum_out=row_sum[:])
+
+        var_eps = [keep.tile([P, 2], F32, name="var_eps01")[:], hid[0][:, 0, 0:2]]
+        rstd = [keep.tile([P, 2], F32, name=f"rstd{h}") for h in range(2)]
+        mean_var = keep.tile([P, last, 2], F32, name="mean_var")
+
+        def moments(t):
+            stats = keep.tile([P, 6], F32, name=f"stats{t}")
+            nc.vector.bn_stats(out=stats[:], in_=jn[t][:])
+            nc.vector.bn_aggr(out=mean_var[:, t, :], in_=stats[:])
+
+        moments(0)
+        moments(1)
+        nc.vector.tensor_scalar(out=var_eps[0], in0=mean_var[:, 0:2, 1], scalar1=EPS, scalar2=None, op0=ALU.add)
+        nc.gpsimd.tensor_tensor(out=rstd[0][:], in0=var_eps[0], in1=minus_half[:], op=ALU.pow)
+        moments(2)
+        nc.vector.tensor_scalar(out=var_eps[1][:, 0:1], in0=mean_var[:, 2, 1:2], scalar1=EPS, scalar2=None, op0=ALU.add)
+        nc.scalar.activation(out=minus_mean[:], in_=row_sum[:], func=ACT.Copy, scale=-1.0 / S)
+        nc.scalar.activation(out=window[0][:, :S], in_=jn[last][:], func=ACT.Square, bias=minus_mean[:], accum_out=square_sum[:])
+        nc.scalar.activation(out=var_eps[1][:, 1:2], in_=square_sum[:], func=ACT.Copy, scale=1.0 / S, bias=EPS)
+        nc.gpsimd.tensor_tensor(out=rstd[1][:], in0=var_eps[1], in1=minus_half[:], op=ALU.pow)
+
+        for t in range(last):
+            nc.scalar.activation(out=pair[:, t, 1:2], in_=minus_unit[:, t : t + 1], func=ACT.Copy, scale=mean_var[:, t, 0:1])
+        nc.scalar.activation(out=pair[:, last, 1:2], in_=unit_sb[:, last:], func=ACT.Copy, scale=minus_mean[:])
+        for h in range(2):
+            for t in (2 * h, 2 * h + 1):
+                nc.scalar.activation(out=affine[:, t, :], in_=pair[:, t, :], func=ACT.Copy, scale=rstd[h][:, t % 2 : t % 2 + 1])
+            for t in (2 * h, 2 * h + 1):
+                nc.scalar.activation(out=window[t][:, :S], in_=jn[t][:], func=ACT.Identity, scale=affine[:, t, 0:1], bias=affine[:, t, 1:2])
+
         gate = keep.tile([P, U], F32, name="gate")
+        nc.scalar.activation(out=gate[:], in_=res_sb[:], func=ACT.Tanh)
 
         starts = [sum(CHUNKS[:c]) for c in range(len(CHUNKS))]
         grouped = {}
@@ -184,20 +186,25 @@ def tile_picked_ymtph_gate_p_kernel(tc, x_words, x_scales, w1, e_words, e_scales
 
         def fetch(c):
             r0, n = starts[c], CHUNKS[c]
-            hid = keep.tile([P, PACK, n], F32, name=f"hid{c}")
             for t in range(PACK):
-                nc.vector.tensor_tensor(out=hid[:, t, :], in0=window[t][:].indirect(par_sb[:, r0 // 16 : (r0 + n) // 16]),
+                nc.vector.tensor_tensor(out=hid[c][:, t, :], in0=window[t][:].indirect(par_sb[:, r0 // 16 : (r0 + n) // 16]),
                                         in1=mod_sb[t][:, r0 : r0 + n], op=ALU.mult)
             grouped[c] = keep.tile([P, n * PACK], BF16, name=f"hid_grouped{c}", align_bytes=64)
-            nc.scalar.copy(out=grouped[c][:].rearrange("p (c i t) -> p c t i", i=4, t=PACK), in_=hid[:].rearrange("p t (c i) -> p c t i", i=4))
-            nc.scalar.activation(out=gate[:, r0 : r0 + n], in_=res_sb[:, r0 : r0 + n], func=ACT.Tanh)
+            nc.scalar.copy(out=grouped[c][:].rearrange("p (c i t) -> p c t i", i=4, t=PACK), in_=hid[c][:].rearrange("p t (c i) -> p c t i", i=4))
 
         def project(c):
             n = CHUNKS[c]
-            codes, scales = quantize(grouped[c], n, f"hid{c}")
+            codes = keep.tile([P, n], U32, name=f"hid_codes{c}", align_bytes=64)
+            scales = keep.tile([P, n], U8, name=f"hid_scales{c}", align_bytes=64)
             product[c] = psum_out.tile([P, n], F32, name="rr")
-            nc.tensor.matmul_mx(out=product[c][:], lhsT=w3_codes[:].bitcast(FP8X4), lhsT_scale=w3_scales[:],
-                                rhs=codes[:].bitcast(FP8X4), rhs_scale=scales[:], start=True, stop=True)
+            a = 0
+            for width in (512, 256, 128):
+                if n & width:
+                    cols = slice(a, a + width)
+                    nc.vector.quantize_mx(out=codes[:, cols].bitcast(FP8X4), scales=scales[:, cols], in_=grouped[c][:, PACK * a : PACK * (a + width)])
+                    nc.tensor.matmul_mx(out=product[c][:, cols], lhsT=w3_codes[:].bitcast(FP8X4), lhsT_scale=w3_scales[:],
+                                        rhs=codes[:, cols].bitcast(FP8X4), rhs_scale=scales[:, cols], start=True, stop=True)
+                    a = a + width
 
         def finish(c):
             r0, n = starts[c], CHUNKS[c]

@@ -17,8 +17,12 @@ ACT = mybir.ActivationFunctionType
 
 P = 128
 PACK = 4
+EARLY = 2
+GROUP = 16
 EPS = 0.1
-CHUNKS = (512, 384, 128)
+CHUNK = 256
+ORDER = (1, 2, 3, 0)
+AHEAD = 640
 SPARE = 32
 VECTOR_SHARE = 40
 
@@ -27,73 +31,74 @@ def tile_picked_ymtph_gate_p_kernel(tc, x_words, x_scales, w1, e_words, e_scales
     nc = tc.nc
     with ExitStack() as ctx:
         keep = ctx.enter_context(tc.tile_pool(name="keep", bufs=1))
-        psum = ctx.enter_context(tc.psum_pool(name="psum", bufs=1))
-        psum_out = ctx.enter_context(tc.psum_pool(name="psum_out", bufs=3))
+        psum_pre = ctx.enter_context(tc.psum_pool(name="psum_pre", bufs=1))
+        psum_out = ctx.enter_context(tc.psum_pool(name="psum_out", bufs=2))
 
-        offs_sb = keep.tile([P, S // 16], U16, name="offs_sb")
-        nxt_sb = keep.tile([P, S // 16], U16, name="nxt_sb")
-        par_sb = keep.tile([P, U // 16], U16, name="par_sb")
-        xs_tab = keep.tile([P, T], U8, name="xs_tab", align_bytes=64)
-        es_tab = keep.tile([P, W], U8, name="es_tab", align_bytes=64)
-        xw_tab = keep.tile([P, T], U32, name="xw_tab", align_bytes=64)
-        ew_tab = keep.tile([P, W], U32, name="ew_tab", align_bytes=64)
-        w1_raw = [keep.tile([P, PACK, H // 2], F32, name=f"w1_raw{h}") for h in range(2)]
-        w2_raw = [keep.tile([P, PACK, H // 2], F32, name=f"w2_raw{h}") for h in range(2)]
+        offs_sb = keep.tile([P, S // GROUP], U16, name="offs_sb")
+        nxt_sb = keep.tile([P, S // GROUP], U16, name="nxt_sb")
+        par_sb = keep.tile([P, U // GROUP], U16, name="par_sb")
+        x_scale_table = keep.tile([P, T], U8, name="x_scale_table", align_bytes=64)
+        e_scale_table = keep.tile([P, W], U8, name="e_scale_table", align_bytes=64)
+        x_word_table = keep.tile([P, T], U32, name="x_word_table", align_bytes=64)
+        e_word_table = keep.tile([P, W], U32, name="e_word_table", align_bytes=64)
+        w1_pieces = [keep.tile([P, PACK, H], F32, name="w1_raw")]
+        w2_pieces = [keep.tile([P, PACK, H // 2], F32, name=f"w2_raw{h}") for h in range(2)]
         w3_raw = keep.tile([P, PACK, N], F32, name="w3_raw")
         unit_sb = keep.tile([P, PACK], F32, name="unit_sb")
-        mod_sb = [keep.tile([P, U], F32, name=f"mod_sb{t}") for t in range(PACK)]
+        mod_sb = [keep.tile([P, U], F32, name=f"mod_sb{t}") for t in range(PACK - 1)]
+        hid = [keep.tile([P, PACK, CHUNK], F32, name=f"hid{c}") for c in range(U // CHUNK)]
+        mod_tail = keep.tile([P, CHUNK], F32, name="mod_tail")
+        mod_slot3 = dict(zip(ORDER, [hid[c][:, 2, :] for c in ORDER[1:]] + [mod_tail[:]]))
         res_sb = keep.tile([P, U], F32, name="res_sb")
-        minus_half = keep.tile([P, 2], F32, name="minus_half")
+        minus_half = keep.tile([P, PACK], F32, name="minus_half")
 
-        nc.gpsimd.memset(xs_tab[:].bitcast(I32), 0)
-        nc.vector.memset(es_tab[:].bitcast(I32), 0)
+        nc.gpsimd.memset(x_scale_table[:].bitcast(I32), 0)
+        nc.vector.memset(e_scale_table[:].bitcast(I32), 0)
         nc.gpsimd.memset(minus_half[:], -0.5)
 
-        def load_scales(tab, scales):
+        def load_scales(table, scales):
             for q in range(4):
-                nc.sync.dma_start(out=tab[32 * q : 32 * q + 4, :].bitcast(I32), in_=scales[0, 4 * q : 4 * q + 4, :].bitcast(I32))
+                nc.sync.dma_start(out=table[32 * q : 32 * q + 4, :].bitcast(I32), in_=scales[0, 4 * q : 4 * q + 4, :].bitcast(I32))
 
-        def load_words(tab, words):
-            nc.sync.dma_start(out=tab[:].bitcast(I32), in_=words[0].rearrange("p n j -> p (n j)").bitcast(I32))
+        def load_words(table, words):
+            nc.sync.dma_start(out=table[:].bitcast(I32), in_=words[0].rearrange("p n j -> p (n j)").bitcast(I32))
 
-        def load_weight(halves, w):
+        def load_weight(pieces, w):
             rows = w.rearrange("(p j) c -> p j c", j=PACK)
-            for h in range(2):
-                nc.sync.dma_start(out=halves[h][:], in_=rows[:, :, h * H // 2 : (h + 1) * H // 2])
+            width = H // len(pieces)
+            for h, piece in enumerate(pieces):
+                nc.sync.dma_start(out=piece[:], in_=rows[:, :, h * width : (h + 1) * width])
 
         nc.sync.dma_start(out=offs_sb[:], in_=offs)
         nc.sync.dma_start(out=nxt_sb[:], in_=nxt)
-        load_words(xw_tab, x_words)
-        load_scales(xs_tab, x_scales)
-        load_weight(w1_raw, w1)
-        load_scales(es_tab, e_scales)
-        load_words(ew_tab, e_words)
-        load_weight(w2_raw, w2)
+        load_words(x_word_table, x_words)
+        load_scales(x_scale_table, x_scales)
+        load_weight(w1_pieces, w1)
+        load_scales(e_scale_table, e_scales)
+        load_words(e_word_table, e_words)
         nc.sync.dma_start(out=unit_sb[:], in_=unit.rearrange("(p t) o -> p (t o)", t=PACK))
+        load_weight(w2_pieces, w2)
         nc.sync.dma_start(out=w3_raw[:], in_=w3.rearrange("(p j) c -> p j c", j=PACK))
         nc.sync.dma_start(out=par_sb[:], in_=par)
         mod_rows = mod.rearrange("(p t) r -> p t r", t=PACK)
-        for t in range(PACK):
+        for t in range(PACK - 1):
             nc.sync.dma_start(out=mod_sb[t][:], in_=mod_rows[:, t, :])
+        for c in ORDER:
+            nc.sync.dma_start(out=mod_slot3[c], in_=mod_rows[:, PACK - 1, c * CHUNK : (c + 1) * CHUNK])
         nc.sync.dma_start(out=res_sb[:], in_=res)
 
-        def gather_scales(tab, lst, name):
-            picked = keep.tile([P, S], U8, name=name, align_bytes=64)
-            nc.vector.tensor_copy(out=picked[:], in_=tab[:].indirect(lst[:]))
+        def pick(table, entries, dtype, name):
+            picked = keep.tile([P, S], dtype, name=name, align_bytes=64)
+            nc.vector.tensor_copy(out=picked[:], in_=table[:].indirect(entries[:]))
             return picked
 
-        def gather_words(tab, lst, name):
-            picked = keep.tile([P, S], U32, name=name, align_bytes=64)
-            nc.vector.tensor_copy(out=picked[:], in_=tab[:].indirect(lst[:]))
-            return picked
-
-        def deal(halves, name, vector_shares):
+        def deal(pieces, name, share):
             grouped = keep.tile([P, PACK * H], BF16, name=name, align_bytes=64)
-            dealt = grouped[:].rearrange("p (t m j) -> p m j t", t=PACK, j=PACK)
-            for h in range(2):
-                dst = dealt[:, h * P // 2 : (h + 1) * P // 2]
-                src = halves[h][:].rearrange("p j (m t) -> p m j t", t=PACK)
-                share = vector_shares[h]
+            dealt = grouped[:].rearrange("p (t m j) -> p m t j", t=PACK, j=PACK)
+            width = P // len(pieces)
+            for h, piece in enumerate(pieces):
+                dst = dealt[:, h * width : (h + 1) * width]
+                src = piece[:].rearrange("p j (m t) -> p m t j", t=PACK)
                 if share:
                     nc.vector.tensor_copy(out=dst[:, :share], in_=src[:, :share])
                 nc.scalar.copy(out=dst[:, share:], in_=src[:, share:])
@@ -105,119 +110,130 @@ def tile_picked_ymtph_gate_p_kernel(tc, x_words, x_scales, w1, e_words, e_scales
             nc.vector.quantize_mx(out=codes[:].bitcast(FP8X4), scales=scales[:], in_=grouped[:])
             return codes, scales
 
-        xw = gather_words(xw_tab, offs_sb, "xw")
-        xs = gather_scales(xs_tab, offs_sb, "xs")
-        w1_grouped = deal(w1_raw, "w1_grouped", (0, 0))
-        es = gather_scales(es_tab, nxt_sb, "es")
+        def side_by_side(grouped, rows):
+            return grouped[:].rearrange("p (c i j) -> p c j i", i=4, j=PACK), rows[:].rearrange("p j (c i) -> p c j i", i=4)
+
+        x_picked_words = pick(x_word_table, offs_sb, U32, "x_picked_words")
+        x_picked_scales = pick(x_scale_table, offs_sb, U8, "x_picked_scales")
+        w1_grouped = deal(w1_pieces, "w1_grouped", 0)
+        e_picked_scales = pick(e_scale_table, nxt_sb, U8, "e_picked_scales")
         w1_codes, w1_scales = quantize(w1_grouped, H, "w1")
-        ew = gather_words(ew_tab, nxt_sb, "ew")
-        w2_grouped = deal(w2_raw, "w2_grouped", (VECTOR_SHARE, VECTOR_SHARE))
+        e_picked_words = pick(e_word_table, nxt_sb, U32, "e_picked_words")
+        w2_grouped = deal(w2_pieces, "w2_grouped", VECTOR_SHARE)
         w2_codes = keep.tile([P, H], U32, name="w2_codes", align_bytes=64)
         w2_scales = keep.tile([P, H], U8, name="w2_scales", align_bytes=64)
         for t in range(PACK):
             cols = slice(P * t, P * (t + 1))
             nc.vector.quantize_mx(out=w2_codes[:, cols].bitcast(FP8X4), scales=w2_scales[:, cols], in_=w2_grouped[:, H * t : H * (t + 1)])
 
-        pre = [psum.tile([P, S], F32, name=f"pre{t}") for t in range(PACK)]
+        pre = [psum_pre.tile([P, S], F32, name=f"pre{t}") for t in range(PACK)]
+        passes = ((w1_codes, w1_scales, x_picked_words, x_picked_scales), (w2_codes, w2_scales, e_picked_words, e_picked_scales))
         for t in range(PACK):
             cols = slice(P * t, P * (t + 1))
-            for codes, scales, words, byts, first in ((w1_codes, w1_scales, xw, xs, True), (w2_codes, w2_scales, ew, es, False)):
-                nc.tensor.matmul_mx(out=pre[t][:], lhsT=codes[:, cols].bitcast(FP8X4), lhsT_scale=scales[:, cols],
-                                    rhs=words[:].bitcast(FP8X4), rhs_scale=byts[:], start=first, stop=not first)
+            for g, (w_codes, w_scales, picked_words, picked_scales) in enumerate(passes):
+                nc.tensor.matmul_mx(out=pre[t][:], lhsT=w_codes[:, cols].bitcast(FP8X4), lhsT_scale=w_scales[:, cols],
+                                    rhs=picked_words[:].bitcast(FP8X4), rhs_scale=picked_scales[:], start=g == 0, stop=g == len(passes) - 1)
 
         w3_grouped = keep.tile([P, N * PACK], BF16, name="w3_grouped", align_bytes=64)
-        nc.scalar.copy(out=w3_grouped[:].rearrange("p (c i j) -> p c j i", i=4, j=PACK), in_=w3_raw[:].rearrange("p j (c i) -> p c j i", i=4))
+        w3_dst, w3_src = side_by_side(w3_grouped, w3_raw)
+        nc.vector.tensor_copy(out=w3_dst, in_=w3_src)
         w3_codes, w3_scales = quantize(w3_grouped, N, "w3")
 
         jn = [keep.tile([P, S], F32, name=f"jn{t}") for t in range(PACK)]
-        window = [keep.tile([P, S + SPARE], F32, name=f"window{t}") for t in range(PACK)]
-        for t in range(PACK):
+        window = [keep.tile([P, width], F32, name=f"window{t}") for t, width in enumerate((U + SPARE, AHEAD + SPARE, S, S))]
+        unscaled = [keep.tile([P, U], F32, name=f"unscaled{t}") for t in range(EARLY)]
+        for t in range(EARLY):
             nc.gpsimd.memset(window[t][:, S:], 0.0)
-        hid = [keep.tile([P, PACK, n], F32, name=f"hid{c}") for c, n in enumerate(CHUNKS)]
-        last = PACK - 1
-        row_sum = keep.tile([P, 1], F32, name="row_sum")
-        minus_mean = keep.tile([P, 1], F32, name="minus_mean")
-        square_sum = keep.tile([P, 1], F32, name="square_sum")
-        minus_unit = keep.tile([P, PACK], F32, name="minus_unit")
-        pair = keep.tile([P, PACK, 2], F32, name="pair")
-        affine = keep.tile([P, PACK, 2], F32, name="affine")
-        nc.scalar.activation(out=minus_unit[:], in_=unit_sb[:], func=ACT.Copy, scale=-1.0)
-        nc.scalar.copy(out=pair[:, :, 0], in_=unit_sb[:])
+        row_sum = keep.tile([P, PACK], F32, name="row_sum")
+        tanh_res = keep.tile([P, U], F32, name="tanh_res")
+        squares = tanh_res[:, :S]
+        square_sum = tanh_res[:, S : S + PACK]
+        minus_unit_share = keep.tile([P, PACK], F32, name="minus_unit_share")
+        pair = keep.tile([P, PACK - EARLY, 2], F32, name="pair")
+        affine = keep.tile([P, PACK - EARLY, 2], F32, name="affine")
+        late_factor = keep.tile([P, EARLY], F32, name="late_factor")
+        rstd = keep.tile([P, PACK], F32, name="rstd")
+        var_eps = unscaled[1][:, AHEAD : AHEAD + PACK]
+        nc.scalar.activation(out=minus_unit_share[:], in_=unit_sb[:], func=ACT.Copy, scale=-1.0 / S)
+        nc.scalar.copy(out=pair[:, :, 0], in_=unit_sb[:, EARLY:])
 
-        for t in range(last):
-            nc.scalar.activation(out=jn[t][:], in_=pre[t][:], func=ACT.Gelu_apprx_tanh)
-        nc.scalar.activation(out=jn[last][:], in_=pre[last][:], func=ACT.Gelu_apprx_tanh, accum_out=row_sum[:])
+        def fetch(dst, t, r0, n, factor):
+            nc.vector.tensor_tensor(out=dst, in0=window[t][:].indirect(par_sb[:, r0 // GROUP : (r0 + n) // GROUP]), in1=factor, op=ALU.mult)
 
-        var_eps = [keep.tile([P, 2], F32, name="var_eps01")[:], hid[0][:, 0, 0:2]]
-        rstd = [keep.tile([P, 2], F32, name=f"rstd{h}") for h in range(2)]
-        mean_var = keep.tile([P, last, 2], F32, name="mean_var")
+        def centre(t):
+            nc.vector.tensor_scalar(out=window[t][:, :S], in0=jn[t][:], scalar1=-float(S), scalar2=row_sum[:, t : t + 1], op0=ALU.mult, op1=ALU.add)
 
-        def moments(t):
-            stats = keep.tile([P, 6], F32, name=f"stats{t}")
-            nc.vector.bn_stats(out=stats[:], in_=jn[t][:])
-            nc.vector.bn_aggr(out=mean_var[:, t, :], in_=stats[:])
+        for t in range(PACK):
+            nc.scalar.activation(out=jn[t][:], in_=pre[t][:], func=ACT.Gelu_apprx_tanh, accum_out=row_sum[:, t : t + 1])
+        centre(0)
+        fetch(unscaled[0][:], 0, 0, U, mod_sb[0][:])
+        centre(1)
+        fetch(unscaled[1][:, :AHEAD], 1, 0, AHEAD, mod_sb[1][:, :AHEAD])
+        for t in range(PACK):
+            nc.scalar.activation(out=squares, in_=jn[t][:], func=ACT.Square, scale=-float(S), bias=row_sum[:, t : t + 1], accum_out=square_sum[:, t : t + 1])
+        nc.scalar.activation(out=var_eps, in_=square_sum, func=ACT.Copy, scale=1.0 / S**3, bias=EPS)
+        nc.gpsimd.tensor_tensor(out=rstd[:], in0=var_eps, in1=minus_half[:], op=ALU.pow)
 
-        moments(0)
-        moments(1)
-        nc.vector.tensor_scalar(out=var_eps[0], in0=mean_var[:, 0:2, 1], scalar1=EPS, scalar2=None, op0=ALU.add)
-        nc.gpsimd.tensor_tensor(out=rstd[0][:], in0=var_eps[0], in1=minus_half[:], op=ALU.pow)
-        moments(2)
-        nc.vector.tensor_scalar(out=var_eps[1][:, 0:1], in0=mean_var[:, 2, 1:2], scalar1=EPS, scalar2=None, op0=ALU.add)
-        nc.scalar.activation(out=minus_mean[:], in_=row_sum[:], func=ACT.Copy, scale=-1.0 / S)
-        nc.scalar.activation(out=window[0][:, :S], in_=jn[last][:], func=ACT.Square, bias=minus_mean[:], accum_out=square_sum[:])
-        nc.scalar.activation(out=var_eps[1][:, 1:2], in_=square_sum[:], func=ACT.Copy, scale=1.0 / S, bias=EPS)
-        nc.gpsimd.tensor_tensor(out=rstd[1][:], in0=var_eps[1], in1=minus_half[:], op=ALU.pow)
+        for t in range(EARLY, PACK):
+            nc.scalar.activation(out=pair[:, t - EARLY, 1:2], in_=minus_unit_share[:, t : t + 1], func=ACT.Copy, scale=row_sum[:, t : t + 1])
+        fetch(unscaled[1][:, AHEAD:], 1, AHEAD, U - AHEAD, mod_sb[1][:, AHEAD:])
+        for t in range(EARLY, PACK):
+            nc.scalar.activation(out=affine[:, t - EARLY, :], in_=pair[:, t - EARLY, :], func=ACT.Copy, scale=rstd[:, t : t + 1])
+        for t in range(EARLY, PACK):
+            nc.scalar.activation(out=window[t][:], in_=jn[t][:], func=ACT.Identity, scale=affine[:, t - EARLY, 0:1], bias=affine[:, t - EARLY, 1:2])
+        for t in range(EARLY):
+            nc.scalar.activation(out=late_factor[:, t : t + 1], in_=minus_unit_share[:, t : t + 1], func=ACT.Copy, scale=rstd[:, t : t + 1])
 
-        for t in range(last):
-            nc.scalar.activation(out=pair[:, t, 1:2], in_=minus_unit[:, t : t + 1], func=ACT.Copy, scale=mean_var[:, t, 0:1])
-        nc.scalar.activation(out=pair[:, last, 1:2], in_=unit_sb[:, last:], func=ACT.Copy, scale=minus_mean[:])
-        for h in range(2):
-            for t in (2 * h, 2 * h + 1):
-                nc.scalar.activation(out=affine[:, t, :], in_=pair[:, t, :], func=ACT.Copy, scale=rstd[h][:, t % 2 : t % 2 + 1])
-            for t in (2 * h, 2 * h + 1):
-                nc.scalar.activation(out=window[t][:, :S], in_=jn[t][:], func=ACT.Identity, scale=affine[:, t, 0:1], bias=affine[:, t, 1:2])
+        nc.scalar.activation(out=tanh_res[:], in_=res_sb[:], func=ACT.Tanh)
 
-        gate = keep.tile([P, U], F32, name="gate")
-        nc.scalar.activation(out=gate[:], in_=res_sb[:], func=ACT.Tanh)
+        hid_grouped = [keep.tile([P, CHUNK * PACK], BF16, name=f"hid_grouped{c}", align_bytes=64) for c in range(U // CHUNK)]
+        half = U // 2
+        rr = [psum_out.tile([P, half], F32, name="rr") for h in range(2)]
 
-        starts = [sum(CHUNKS[:c]) for c in range(len(CHUNKS))]
-        grouped = {}
-        product = {}
+        def rescale(c):
+            for t in range(EARLY):
+                nc.scalar.activation(out=hid[c][:, t, :], in_=unscaled[t][:, c * CHUNK : (c + 1) * CHUNK], func=ACT.Copy, scale=late_factor[:, t : t + 1])
 
-        def fetch(c):
-            r0, n = starts[c], CHUNKS[c]
-            for t in range(PACK):
-                nc.vector.tensor_tensor(out=hid[c][:, t, :], in0=window[t][:].indirect(par_sb[:, r0 // 16 : (r0 + n) // 16]),
-                                        in1=mod_sb[t][:, r0 : r0 + n], op=ALU.mult)
-            grouped[c] = keep.tile([P, n * PACK], BF16, name=f"hid_grouped{c}", align_bytes=64)
-            nc.scalar.copy(out=grouped[c][:].rearrange("p (c i t) -> p c t i", i=4, t=PACK), in_=hid[c][:].rearrange("p t (c i) -> p c t i", i=4))
+        def weave(c):
+            fetch(hid[c][:, 2, :], 2, c * CHUNK, CHUNK, mod_sb[2][:, c * CHUNK : (c + 1) * CHUNK])
+            fetch(hid[c][:, 3, :], 3, c * CHUNK, CHUNK, mod_slot3[c])
+            dst, src = side_by_side(hid_grouped[c], hid[c])
+            if c == ORDER[-1]:
+                nc.vector.tensor_copy(out=dst, in_=src)
+            else:
+                nc.scalar.copy(out=dst, in_=src)
 
         def project(c):
-            n = CHUNKS[c]
-            codes = keep.tile([P, n], U32, name=f"hid_codes{c}", align_bytes=64)
-            scales = keep.tile([P, n], U8, name=f"hid_scales{c}", align_bytes=64)
-            product[c] = psum_out.tile([P, n], F32, name="rr")
-            a = 0
-            for width in (512, 256, 128):
-                if n & width:
-                    cols = slice(a, a + width)
-                    nc.vector.quantize_mx(out=codes[:, cols].bitcast(FP8X4), scales=scales[:, cols], in_=grouped[c][:, PACK * a : PACK * (a + width)])
-                    nc.tensor.matmul_mx(out=product[c][:, cols], lhsT=w3_codes[:].bitcast(FP8X4), lhsT_scale=w3_scales[:],
-                                        rhs=codes[:, cols].bitcast(FP8X4), rhs_scale=scales[:, cols], start=True, stop=True)
-                    a = a + width
+            codes, scales = quantize(hid_grouped[c], CHUNK, f"hid{c}")
+            h, a = divmod(c * CHUNK, half)
+            nc.tensor.matmul_mx(out=rr[h][:, a : a + CHUNK], lhsT=w3_codes[:].bitcast(FP8X4), lhsT_scale=w3_scales[:],
+                                rhs=codes[:].bitcast(FP8X4), rhs_scale=scales[:], start=True, stop=True)
 
-        def finish(c):
-            r0, n = starts[c], CHUNKS[c]
-            gated = keep.tile([P, n], F32, name=f"gated{c}")
-            result = keep.tile([P, n], F32, name=f"result{c}")
-            nc.vector.scalar_tensor_tensor(out=gated[:], in0=gate[:, r0 : r0 + n], scalar=1.0, in1=product[c][:], op0=ALU.add, op1=ALU.mult)
-            nc.vector.scalar_tensor_tensor(out=result[:], in0=gated[:], scalar=0.5, in1=res_sb[:, r0 : r0 + n], op0=ALU.mult, op1=ALU.add)
-            nc.sync.dma_start(out=out[:, r0 : r0 + n], in_=result[:])
+        def gate(h, gated):
+            nc.vector.scalar_tensor_tensor(out=gated, in0=tanh_res[:, h * half : (h + 1) * half], scalar=1.0, in1=rr[h][:], op0=ALU.add, op1=ALU.mult)
 
-        for step in range(len(CHUNKS) + 2):
-            if step < len(CHUNKS):
-                fetch(step)
-            if 1 <= step <= len(CHUNKS):
-                project(step - 1)
-            if step >= 2:
-                finish(step - 2)
+        def finish(gated, result, r0, n):
+            nc.vector.scalar_tensor_tensor(out=result, in0=gated, scalar=0.5, in1=res_sb[:, r0 : r0 + n], op0=ALU.mult, op1=ALU.add)
+            nc.sync.dma_start(out=out[:, r0 : r0 + n], in_=result)
+
+        first, second, third, last = ORDER
+        rescale(first)
+        weave(first)
+        rescale(second)
+        rescale(last)
+        weave(second)
+        rescale(third)
+        weave(third)
+        weave(last)
+
+        for c in (last, first, second):
+            project(c)
+        gated_low = hid_grouped[second][:].bitcast(F32)
+        gate(0, gated_low)
+        project(third)
+        finish(gated_low, hid_grouped[third][:].bitcast(F32), 0, half)
+        gated_high = keep.tile([P, half], F32, name="gated_high")
+        result_high = keep.tile([P, half], F32, name="result_high")
+        gate(1, gated_high[:])
+        for a in range(0, half, CHUNK):
+            finish(gated_high[:, a : a + CHUNK], result_high[:, a : a + CHUNK], half + a, CHUNK)

from contextlib import ExitStack

import concourse.mybir as mybir

K, T, S, N, H, W, U = 512, 1024, 512, 128, 512, 2048, 1024
FLOPS = 2 * K * H * S * 2 + 2 * H * N * U

F32 = mybir.dt.float32
BF16 = mybir.dt.bfloat16
I32 = mybir.dt.int32
U32 = mybir.dt.uint32
U16 = mybir.dt.uint16
U8 = mybir.dt.uint8
FP8X4 = mybir.dt.float8_e4m3fn_x4
ALU = mybir.AluOpType
ACT = mybir.ActivationFunctionType

P = 128
PACK = 4
EARLY = 2
GROUP = 16
EPS = 0.1
CHUNK = 256
ORDER = (1, 2, 3, 0)
AHEAD = 640
SPARE = 32
VECTOR_SHARE = 40


def tile_picked_ymtph_gate_p_kernel(tc, x_words, x_scales, w1, e_words, e_scales, w2, mod, unit, w3, res, offs, nxt, par, out):
    nc = tc.nc
    with ExitStack() as ctx:
        keep = ctx.enter_context(tc.tile_pool(name="keep", bufs=1))
        psum_pre = ctx.enter_context(tc.psum_pool(name="psum_pre", bufs=1))
        psum_out = ctx.enter_context(tc.psum_pool(name="psum_out", bufs=2))

        offs_sb = keep.tile([P, S // GROUP], U16, name="offs_sb")
        nxt_sb = keep.tile([P, S // GROUP], U16, name="nxt_sb")
        par_sb = keep.tile([P, U // GROUP], U16, name="par_sb")
        x_scale_table = keep.tile([P, T], U8, name="x_scale_table", align_bytes=64)
        e_scale_table = keep.tile([P, W], U8, name="e_scale_table", align_bytes=64)
        x_word_table = keep.tile([P, T], U32, name="x_word_table", align_bytes=64)
        e_word_table = keep.tile([P, W], U32, name="e_word_table", align_bytes=64)
        w1_pieces = [keep.tile([P, PACK, H], F32, name="w1_raw")]
        w2_pieces = [keep.tile([P, PACK, H // 2], F32, name=f"w2_raw{h}") for h in range(2)]
        w3_raw = keep.tile([P, PACK, N], F32, name="w3_raw")
        unit_sb = keep.tile([P, PACK], F32, name="unit_sb")
        mod_sb = [keep.tile([P, U], F32, name=f"mod_sb{t}") for t in range(PACK - 1)]
        hid = [keep.tile([P, PACK, CHUNK], F32, name=f"hid{c}") for c in range(U // CHUNK)]
        mod_tail = keep.tile([P, CHUNK], F32, name="mod_tail")
        mod_slot3 = dict(zip(ORDER, [hid[c][:, 2, :] for c in ORDER[1:]] + [mod_tail[:]]))
        res_sb = keep.tile([P, U], F32, name="res_sb")
        minus_half = keep.tile([P, PACK], F32, name="minus_half")

        nc.gpsimd.memset(x_scale_table[:].bitcast(I32), 0)
        nc.vector.memset(e_scale_table[:].bitcast(I32), 0)
        nc.gpsimd.memset(minus_half[:], -0.5)

        def load_scales(table, scales):
            for q in range(4):
                nc.sync.dma_start(out=table[32 * q : 32 * q + 4, :].bitcast(I32), in_=scales[0, 4 * q : 4 * q + 4, :].bitcast(I32))

        def load_words(table, words):
            nc.sync.dma_start(out=table[:].bitcast(I32), in_=words[0].rearrange("p n j -> p (n j)").bitcast(I32))

        def load_weight(pieces, w):
            rows = w.rearrange("(p j) c -> p j c", j=PACK)
            width = H // len(pieces)
            for h, piece in enumerate(pieces):
                nc.sync.dma_start(out=piece[:], in_=rows[:, :, h * width : (h + 1) * width])

        nc.sync.dma_start(out=offs_sb[:], in_=offs)
        nc.sync.dma_start(out=nxt_sb[:], in_=nxt)
        load_words(x_word_table, x_words)
        load_scales(x_scale_table, x_scales)
        load_weight(w1_pieces, w1)
        load_scales(e_scale_table, e_scales)
        load_words(e_word_table, e_words)
        nc.sync.dma_start(out=unit_sb[:], in_=unit.rearrange("(p t) o -> p (t o)", t=PACK))
        load_weight(w2_pieces, w2)
        nc.sync.dma_start(out=w3_raw[:], in_=w3.rearrange("(p j) c -> p j c", j=PACK))
        nc.sync.dma_start(out=par_sb[:], in_=par)
        mod_rows = mod.rearrange("(p t) r -> p t r", t=PACK)
        for t in range(PACK - 1):
            nc.sync.dma_start(out=mod_sb[t][:], in_=mod_rows[:, t, :])
        for c in ORDER:
            nc.sync.dma_start(out=mod_slot3[c], in_=mod_rows[:, PACK - 1, c * CHUNK : (c + 1) * CHUNK])
        nc.sync.dma_start(out=res_sb[:], in_=res)

        def pick(table, entries, dtype, name):
            picked = keep.tile([P, S], dtype, name=name, align_bytes=64)
            nc.vector.tensor_copy(out=picked[:], in_=table[:].indirect(entries[:]))
            return picked

        def deal(pieces, name, share):
            grouped = keep.tile([P, PACK * H], BF16, name=name, align_bytes=64)
            dealt = grouped[:].rearrange("p (t m j) -> p m t j", t=PACK, j=PACK)
            width = P // len(pieces)
            for h, piece in enumerate(pieces):
                dst = dealt[:, h * width : (h + 1) * width]
                src = piece[:].rearrange("p j (m t) -> p m t j", t=PACK)
                if share:
                    nc.vector.tensor_copy(out=dst[:, :share], in_=src[:, :share])
                nc.scalar.copy(out=dst[:, share:], in_=src[:, share:])
            return grouped

        def quantize(grouped, width, name):
            codes = keep.tile([P, width], U32, name=name + "_codes", align_bytes=64)
            scales = keep.tile([P, width], U8, name=name + "_scales", align_bytes=64)
            nc.vector.quantize_mx(out=codes[:].bitcast(FP8X4), scales=scales[:], in_=grouped[:])
            return codes, scales

        def side_by_side(grouped, rows):
            return grouped[:].rearrange("p (c i j) -> p c j i", i=4, j=PACK), rows[:].rearrange("p j (c i) -> p c j i", i=4)

        x_picked_words = pick(x_word_table, offs_sb, U32, "x_picked_words")
        x_picked_scales = pick(x_scale_table, offs_sb, U8, "x_picked_scales")
        w1_grouped = deal(w1_pieces, "w1_grouped", 0)
        e_picked_scales = pick(e_scale_table, nxt_sb, U8, "e_picked_scales")
        w1_codes, w1_scales = quantize(w1_grouped, H, "w1")
        e_picked_words = pick(e_word_table, nxt_sb, U32, "e_picked_words")
        w2_grouped = deal(w2_pieces, "w2_grouped", VECTOR_SHARE)
        w2_codes = keep.tile([P, H], U32, name="w2_codes", align_bytes=64)
        w2_scales = keep.tile([P, H], U8, name="w2_scales", align_bytes=64)
        for t in range(PACK):
            cols = slice(P * t, P * (t + 1))
            nc.vector.quantize_mx(out=w2_codes[:, cols].bitcast(FP8X4), scales=w2_scales[:, cols], in_=w2_grouped[:, H * t : H * (t + 1)])

        pre = [psum_pre.tile([P, S], F32, name=f"pre{t}") for t in range(PACK)]
        passes = ((w1_codes, w1_scales, x_picked_words, x_picked_scales), (w2_codes, w2_scales, e_picked_words, e_picked_scales))
        for t in range(PACK):
            cols = slice(P * t, P * (t + 1))
            for g, (w_codes, w_scales, picked_words, picked_scales) in enumerate(passes):
                nc.tensor.matmul_mx(out=pre[t][:], lhsT=w_codes[:, cols].bitcast(FP8X4), lhsT_scale=w_scales[:, cols],
                                    rhs=picked_words[:].bitcast(FP8X4), rhs_scale=picked_scales[:], start=g == 0, stop=g == len(passes) - 1)

        w3_grouped = keep.tile([P, N * PACK], BF16, name="w3_grouped", align_bytes=64)
        w3_dst, w3_src = side_by_side(w3_grouped, w3_raw)
        nc.vector.tensor_copy(out=w3_dst, in_=w3_src)
        w3_codes, w3_scales = quantize(w3_grouped, N, "w3")

        jn = [keep.tile([P, S], F32, name=f"jn{t}") for t in range(PACK)]
        window = [keep.tile([P, width], F32, name=f"window{t}") for t, width in enumerate((U + SPARE, AHEAD + SPARE, S, S))]
        unscaled = [keep.tile([P, U], F32, name=f"unscaled{t}") for t in range(EARLY)]
        for t in range(EARLY):
            nc.gpsimd.memset(window[t][:, S:], 0.0)
        row_sum = keep.tile([P, PACK], F32, name="row_sum")
        tanh_res = keep.tile([P, U], F32, name="tanh_res")
        squares = tanh_res[:, :S]
        square_sum = tanh_res[:, S : S + PACK]
        minus_unit_share = keep.tile([P, PACK], F32, name="minus_unit_share")
        pair = keep.tile([P, PACK - EARLY, 2], F32, name="pair")
        affine = keep.tile([P, PACK - EARLY, 2], F32, name="affine")
        late_factor = keep.tile([P, EARLY], F32, name="late_factor")
        rstd = keep.tile([P, PACK], F32, name="rstd")
        var_eps = unscaled[1][:, AHEAD : AHEAD + PACK]
        nc.scalar.activation(out=minus_unit_share[:], in_=unit_sb[:], func=ACT.Copy, scale=-1.0 / S)
        nc.scalar.copy(out=pair[:, :, 0], in_=unit_sb[:, EARLY:])

        def fetch(dst, t, r0, n, factor):
            nc.vector.tensor_tensor(out=dst, in0=window[t][:].indirect(par_sb[:, r0 // GROUP : (r0 + n) // GROUP]), in1=factor, op=ALU.mult)

        def centre(t):
            nc.vector.tensor_scalar(out=window[t][:, :S], in0=jn[t][:], scalar1=-float(S), scalar2=row_sum[:, t : t + 1], op0=ALU.mult, op1=ALU.add)

        for t in range(PACK):
            nc.scalar.activation(out=jn[t][:], in_=pre[t][:], func=ACT.Gelu_apprx_tanh, accum_out=row_sum[:, t : t + 1])
        centre(0)
        fetch(unscaled[0][:], 0, 0, U, mod_sb[0][:])
        centre(1)
        fetch(unscaled[1][:, :AHEAD], 1, 0, AHEAD, mod_sb[1][:, :AHEAD])
        for t in range(PACK):
            nc.scalar.activation(out=squares, in_=jn[t][:], func=ACT.Square, scale=-float(S), bias=row_sum[:, t : t + 1], accum_out=square_sum[:, t : t + 1])
        nc.scalar.activation(out=var_eps, in_=square_sum, func=ACT.Copy, scale=1.0 / S**3, bias=EPS)
        nc.gpsimd.tensor_tensor(out=rstd[:], in0=var_eps, in1=minus_half[:], op=ALU.pow)

        for t in range(EARLY, PACK):
            nc.scalar.activation(out=pair[:, t - EARLY, 1:2], in_=minus_unit_share[:, t : t + 1], func=ACT.Copy, scale=row_sum[:, t : t + 1])
        fetch(unscaled[1][:, AHEAD:], 1, AHEAD, U - AHEAD, mod_sb[1][:, AHEAD:])
        for t in range(EARLY, PACK):
            nc.scalar.activation(out=affine[:, t - EARLY, :], in_=pair[:, t - EARLY, :], func=ACT.Copy, scale=rstd[:, t : t + 1])
        for t in range(EARLY, PACK):
            nc.scalar.activation(out=window[t][:], in_=jn[t][:], func=ACT.Identity, scale=affine[:, t - EARLY, 0:1], bias=affine[:, t - EARLY, 1:2])
        for t in range(EARLY):
            nc.scalar.activation(out=late_factor[:, t : t + 1], in_=minus_unit_share[:, t : t + 1], func=ACT.Copy, scale=rstd[:, t : t + 1])

        nc.scalar.activation(out=tanh_res[:], in_=res_sb[:], func=ACT.Tanh)

        hid_grouped = [keep.tile([P, CHUNK * PACK], BF16, name=f"hid_grouped{c}", align_bytes=64) for c in range(U // CHUNK)]
        half = U // 2
        rr = [psum_out.tile([P, half], F32, name="rr") for h in range(2)]

        def rescale(c):
            for t in range(EARLY):
                nc.scalar.activation(out=hid[c][:, t, :], in_=unscaled[t][:, c * CHUNK : (c + 1) * CHUNK], func=ACT.Copy, scale=late_factor[:, t : t + 1])

        def weave(c):
            fetch(hid[c][:, 2, :], 2, c * CHUNK, CHUNK, mod_sb[2][:, c * CHUNK : (c + 1) * CHUNK])
            fetch(hid[c][:, 3, :], 3, c * CHUNK, CHUNK, mod_slot3[c])
            dst, src = side_by_side(hid_grouped[c], hid[c])
            if c == ORDER[-1]:
                nc.vector.tensor_copy(out=dst, in_=src)
            else:
                nc.scalar.copy(out=dst, in_=src)

        def project(c):
            codes, scales = quantize(hid_grouped[c], CHUNK, f"hid{c}")
            h, a = divmod(c * CHUNK, half)
            nc.tensor.matmul_mx(out=rr[h][:, a : a + CHUNK], lhsT=w3_codes[:].bitcast(FP8X4), lhsT_scale=w3_scales[:],
                                rhs=codes[:].bitcast(FP8X4), rhs_scale=scales[:], start=True, stop=True)

        def gate(h, gated):
            nc.vector.scalar_tensor_tensor(out=gated, in0=tanh_res[:, h * half : (h + 1) * half], scalar=1.0, in1=rr[h][:], op0=ALU.add, op1=ALU.mult)

        def finish(gated, result, r0, n):
            nc.vector.scalar_tensor_tensor(out=result, in0=gated, scalar=0.5, in1=res_sb[:, r0 : r0 + n], op0=ALU.mult, op1=ALU.add)
            nc.sync.dma_start(out=out[:, r0 : r0 + n], in_=result)

        first, second, third, last = ORDER
        rescale(first)
        weave(first)
        rescale(second)
        rescale(last)
        weave(second)
        rescale(third)
        weave(third)
        weave(last)

        for c in (last, first, second):
            project(c)
        gated_low = hid_grouped[second][:].bitcast(F32)
        gate(0, gated_low)
        project(third)
        finish(gated_low, hid_grouped[third][:].bitcast(F32), 0, half)
        gated_high = keep.tile([P, half], F32, name="gated_high")
        result_high = keep.tile([P, half], F32, name="result_high")
        gate(1, gated_high[:])
        for a in range(0, half, CHUNK):
            finish(gated_high[:, a : a + CHUNK], result_high[:, a : a + CHUNK], half + a, CHUNK)
